import numpy as np
import ml_dtypes

BF16 = ml_dtypes.bfloat16


def bf(x):
    return np.asarray(x, np.float32).astype(BF16)


def f32(x):
    return np.asarray(x, np.float32)


def f64(x):
    return np.asarray(x).astype(np.float64)


def striped(idx):
    return np.tile(idx.reshape(-1, 16).T, (8, 1))


S, K, M, N, D, V = 4096, 256, 128, 2048, 4, 512


def setup_inputs():
    return {"table": bf(np.random.standard_normal((K, S))), "w": bf(np.random.standard_normal((D, K, M)) / np.sqrt(D * K)), "c": f32(0.2 + 0.8 * np.random.random_sample((1, V))), "offs": striped(np.random.permutation(S)[:N])}


def reference(table, w, c, offs):
    idx = offs[:16].T.reshape(-1)
    x = f64(table)[:, idx]
    y = sum(f64(w)[t].T @ x[:, t * V : (t + 1) * V] for t in range(D))
    return y * f64(c)

@@ -1,0 +1,62 @@
+import concourse.mybir as mybir
+
+BF16, F32, U16 = mybir.dt.bfloat16, mybir.dt.float32, mybir.dt.uint16
+
+P = 128
+S = 4096
+K = 256
+M = 128
+RELATIONS = 4
+V = 512
+K_BLOCKS = K // P
+PIECE_COLS = V // 16
+
+FLOPS = 2 * M * K * RELATIONS * V
+
+
+def tile_gather_matmul_kernel(tc, table, w, c, offs, out):
+    nc = tc.nc
+    with (
+        tc.tile_pool(name="held", bufs=1) as held,
+        tc.psum_pool(name="psum", bufs=1) as psum,
+    ):
+        offsets = held.tile([P, RELATIONS * PIECE_COLS], U16, name="offsets")
+        c_row = held.tile([1, V], F32, name="c_row")
+        windows = [held.tile([P, S], BF16, name="window%d" % b) for b in range(K_BLOCKS)]
+        w_first = held.tile([P, K_BLOCKS, M], BF16, name="w_first")
+        w_rest = [held.tile([P, RELATIONS - 1, M], BF16, name="w_rest%d" % b) for b in range(K_BLOCKS)]
+
+        table_blocks = table.rearrange("(p b) s -> b p s", b=K_BLOCKS)
+        w_rows = w.rearrange("t (p b) m -> p t b m", b=K_BLOCKS)
+
+        nc.sync.dma_start(offsets[:], offs)
+        nc.scalar.dma_start(c_row[:], c)
+        nc.scalar.dma_start(w_first[:], w_rows[:, 0])
+        for b in range(K_BLOCKS):
+            nc.sync.dma_start(windows[b][:], table_blocks[b])
+            nc.sync.dma_start(w_rest[b][:], w_rows[:, 1:RELATIONS, b, :])
+
+        ones_row = held.tile([1, M], F32, name="ones_row")
+        nc.vector.memset(ones_row[:], 1.0)
+        c_bank = psum.tile([P, V], F32, name="c_bank")
+        nc.tensor.matmul(c_bank[:], ones_row[:], c_row[:], start=True, stop=True)
+        c_all = held.tile([P, V], F32, name="c_all")
+        nc.vector.tensor_copy(c_all[:], c_bank[:])
+
+        y = psum.tile([M, V], F32, name="y")
+        last = K_BLOCKS * RELATIONS - 1
+        for b in range(K_BLOCKS):
+            for t in range(RELATIONS):
+                step = b * RELATIONS + t
+                piece = offsets[:, t * PIECE_COLS : (t + 1) * PIECE_COLS]
+                nc.tensor.matmul(
+                    y[:],
+                    w_first[:, b, :] if t == 0 else w_rest[b][:, t - 1, :],
+                    windows[b][:].indirect(piece),
+                    start=(step == 0),
+                    stop=(step == last),
+                )
+
+        scaled = held.tile([M, V], F32, name="scaled")
+        nc.vector.tensor_tensor(scaled[:], y[:], c_all[:], mybir.AluOpType.mult)
+        nc.scalar.dma_start(out, scaled[:])

@@ -10,6 +10,7 @@ RELATIONS = 4
 V = 512
 K_BLOCKS = K // P
 PIECE_COLS = V // 16
+ROW_ALIGN = 256
 
 FLOPS = 2 * M * K * RELATIONS * V
 
@@ -20,11 +21,16 @@ def tile_gather_matmul_kernel(tc, table, w, c, offs, out):
         tc.tile_pool(name="held", bufs=1) as held,
         tc.psum_pool(name="psum", bufs=1) as psum,
     ):
-        offsets = held.tile([P, RELATIONS * PIECE_COLS], U16, name="offsets")
+        offsets = held.tile([P, RELATIONS * PIECE_COLS], U16, name="offsets", align_bytes=ROW_ALIGN)
         c_row = held.tile([1, V], F32, name="c_row")
-        windows = [held.tile([P, S], BF16, name="window%d" % b) for b in range(K_BLOCKS)]
-        w_first = held.tile([P, K_BLOCKS, M], BF16, name="w_first")
-        w_rest = [held.tile([P, RELATIONS - 1, M], BF16, name="w_rest%d" % b) for b in range(K_BLOCKS)]
+        windows = [
+            held.tile([P, S], BF16, name="window%d" % b, align_bytes=ROW_ALIGN) for b in range(K_BLOCKS)
+        ]
+        w_first = held.tile([P, K_BLOCKS, M], BF16, name="w_first", align_bytes=ROW_ALIGN)
+        w_rest = [
+            held.tile([P, RELATIONS - 1, M], BF16, name="w_rest%d" % b, align_bytes=ROW_ALIGN)
+            for b in range(K_BLOCKS)
+        ]
 
         table_blocks = table.rearrange("(p b) s -> b p s", b=K_BLOCKS)
         w_rows = w.rearrange("t (p b) m -> p t b m", b=K_BLOCKS)
@@ -57,6 +63,6 @@ def tile_gather_matmul_kernel(tc, table, w, c, offs, out):
                     stop=(step == last),
                 )
 
-        scaled = held.tile([M, V], F32, name="scaled")
+        scaled = held.tile([M, V], F32, name="scaled", align_bytes=ROW_ALIGN)
         nc.vector.tensor_tensor(scaled[:], y[:], c_all[:], mybir.AluOpType.mult)
         nc.scalar.dma_start(out, scaled[:])

import concourse.mybir as mybir

BF16, F32, U16 = mybir.dt.bfloat16, mybir.dt.float32, mybir.dt.uint16

P = 128
S = 4096
K = 256
M = 128
RELATIONS = 4
V = 512
K_BLOCKS = K // P
PIECE_COLS = V // 16
ROW_ALIGN = 256

FLOPS = 2 * M * K * RELATIONS * V


def tile_gather_matmul_kernel(tc, table, w, c, offs, out):
    nc = tc.nc
    with (
        tc.tile_pool(name="held", bufs=1) as held,
        tc.psum_pool(name="psum", bufs=1) as psum,
    ):
        offsets = held.tile([P, RELATIONS * PIECE_COLS], U16, name="offsets", align_bytes=ROW_ALIGN)
        c_row = held.tile([1, V], F32, name="c_row")
        windows = [
            held.tile([P, S], BF16, name="window%d" % b, align_bytes=ROW_ALIGN) for b in range(K_BLOCKS)
        ]
        w_first = held.tile([P, K_BLOCKS, M], BF16, name="w_first", align_bytes=ROW_ALIGN)
        w_rest = [
            held.tile([P, RELATIONS - 1, M], BF16, name="w_rest%d" % b, align_bytes=ROW_ALIGN)
            for b in range(K_BLOCKS)
        ]

        table_blocks = table.rearrange("(p b) s -> b p s", b=K_BLOCKS)
        w_rows = w.rearrange("t (p b) m -> p t b m", b=K_BLOCKS)

        nc.sync.dma_start(offsets[:], offs)
        nc.scalar.dma_start(c_row[:], c)
        nc.scalar.dma_start(w_first[:], w_rows[:, 0])
        for b in range(K_BLOCKS):
            nc.sync.dma_start(windows[b][:], table_blocks[b])
            nc.sync.dma_start(w_rest[b][:], w_rows[:, 1:RELATIONS, b, :])

        ones_row = held.tile([1, M], F32, name="ones_row")
        nc.vector.memset(ones_row[:], 1.0)
        c_bank = psum.tile([P, V], F32, name="c_bank")
        nc.tensor.matmul(c_bank[:], ones_row[:], c_row[:], start=True, stop=True)
        c_all = held.tile([P, V], F32, name="c_all")
        nc.vector.tensor_copy(c_all[:], c_bank[:])

        y = psum.tile([M, V], F32, name="y")
        last = K_BLOCKS * RELATIONS - 1
        for b in range(K_BLOCKS):
            for t in range(RELATIONS):
                step = b * RELATIONS + t
                piece = offsets[:, t * PIECE_COLS : (t + 1) * PIECE_COLS]
                nc.tensor.matmul(
                    y[:],
                    w_first[:, b, :] if t == 0 else w_rest[b][:, t - 1, :],
                    windows[b][:].indirect(piece),
                    start=(step == 0),
                    stop=(step == last),
                )

        scaled = held.tile([M, V], F32, name="scaled", align_bytes=ROW_ALIGN)
        nc.vector.tensor_tensor(scaled[:], y[:], c_all[:], mybir.AluOpType.mult)
        nc.scalar.dma_start(out, scaled[:])
